import numpy as np
import ml_dtypes


def mxq(x, axis, fmt="e4m3"):
    dtype, down = {"e4m3": (ml_dtypes.float8_e4m3fn, 7), "e5m2": (ml_dtypes.float8_e5m2, 14)}[fmt]
    v = np.moveaxis(np.asarray(x, np.float32).astype(ml_dtypes.bfloat16).astype(np.float64), axis, -1)
    blocks = v.reshape(v.shape[:-1] + (-1, 32))
    amax = np.abs(blocks).max(-1, keepdims=True)
    byte = np.maximum(np.where(amax > 0, np.frexp(amax)[1] - 1 + 127, 0) - down, 1)
    scale = np.exp2(byte - 127.0)
    codes = (blocks / scale).astype(np.float32).astype(dtype).astype(np.float64)
    return np.moveaxis((codes * scale).reshape(v.shape), -1, axis)


WIDE = False


def mx_kscale(k):
    if not WIDE:
        return np.ones(k)
    levels = np.array([10, -10, 5, -5, 0])
    if k % 512:
        return np.exp2(np.random.permutation(np.resize(levels, k // 32))).repeat(32)
    a = np.empty((k // 512, 16))
    for p in range(k // 512):
        a[p, :8] = np.random.permutation(np.resize(levels, 8))
        for g in range(8):
            far = levels[np.abs(levels - a[p, g]) >= 10]
            a[p, g + 8] = far[np.random.randint(len(far))]
    return np.exp2(a.ravel()).repeat(32)


def f64(x):
    return np.asarray(x).astype(np.float64)


def striped8(idx):
    return np.asarray(idx).reshape(8, -1, 16).transpose(0, 2, 1).reshape(128, -1).astype(np.uint16)


def unstriped8(offs):
    return offs.reshape(8, 16, -1).transpose(0, 2, 1).reshape(8, -1).astype(np.int64)


def pick8(x, idx, run):
    r = np.arange(len(x))
    return x[r[:, None], idx[r % (8 * run) // run]]


E2M1 = np.array([0.0, 0.5, 1.0, 1.5, 2.0, 3.0, 4.0, 6.0, -0.0, -0.5, -1.0, -1.5, -2.0, -3.0, -4.0, -6.0])


def pack_weight(w, fmt):
    k, n = w.shape
    w = f64(np.asarray(w, np.float32).astype(ml_dtypes.bfloat16)).reshape(k // 32, 32, n)
    amax = np.abs(w).max(1)
    if fmt == "e4m3":
        byte = np.frexp(amax)[1] - 1 + 127 - 7
    else:
        mant, ex = np.frexp(amax / 6.0)
        byte = np.where(mant > 0.5, ex, ex - 1) + 127
    byte = np.clip(np.where(amax > 0, byte, 1), 1, 254)
    scaled = (w * np.exp2(127.0 - byte)[:, None, :]).reshape(k, n).astype(np.float32)
    by_word = np.ascontiguousarray(scaled.reshape(k // 512, 128, 4, n).transpose(0, 1, 3, 2))
    if fmt == "e4m3":
        words = by_word.astype(ml_dtypes.float8_e4m3fn).view(np.uint8)
    else:
        c = by_word.astype(ml_dtypes.float4_e2m1fn).view(np.uint8) & 0xF
        words = (c[..., 0::2] | (c[..., 1::2] << 4)).reshape(k // 512, 128, 2 * n)
    return np.ascontiguousarray(words), np.ascontiguousarray(byte.astype(np.uint8).reshape(k // 512, 16, n))


def unpack_weight(words, scales, fmt):
    g, _, n = scales.shape
    words = np.ascontiguousarray(words).reshape(g, 128, n, -1)
    if fmt == "e4m3":
        vals = words.view(ml_dtypes.float8_e4m3fn).astype(np.float64)
    else:
        nib = np.empty((g, 128, n, 4), np.uint8)
        nib[..., 0::2] = words & 0xF
        nib[..., 1::2] = words >> 4
        vals = E2M1[nib]
    vals = vals * np.repeat(np.exp2(scales.astype(np.float64) - 127.0), 8, axis=1)[..., None]
    return vals.transpose(0, 1, 3, 2).reshape(g * 512, n)


D, T, I, Q = 512, 1024, 512, 128


def setup_inputs():
    n = np.random.standard_normal
    idx = np.stack([np.random.permutation(T)[:I] for _ in range(8)])
    idx2 = np.stack([np.random.permutation(T)[:I] for _ in range(8)])
    idx3 = np.stack([np.random.permutation(T)[:I] for _ in range(8)])
    idx4 = np.stack([np.random.permutation(T)[:I] for _ in range(8)])
    fd = mx_kscale(D)
    keysp = pack_weight(n((D, T)) / fd[:, None], "e4m3")
    return {
        "query": (n((D, Q)) * 1.0 / np.sqrt(D) * fd[:, None]).astype(np.float32),
        "keys_words": keysp[0],
        "keys_scales": keysp[1],
        "lam": (np.random.uniform(0.4, 1.0, (Q, 1))).astype(np.float32),
        "old": (1.0 * n((Q, T))).astype(np.float32),
        "offs": striped8(idx),
        "offs2": striped8(idx2),
        "offs3": striped8(idx3),
        "offs4": striped8(idx4),
    }


def reference(query, keys_words, keys_scales, lam, old, offs, offs2, offs3, offs4):
    idx = unstriped8(offs)
    idx2 = unstriped8(offs2)
    idx3 = unstriped8(offs3)
    idx4 = unstriped8(offs4)
    keysu = unpack_weight(keys_words, keys_scales, "e4m3")
    queryq = mxq(f64(query), 0, "e4m3")
    a = queryq.T @ keysu
    w = pick8(a, idx, 16) + np.tanh(pick8(a, idx2, 16) - pick8(a, idx3, 16)) * f64(lam)
    f1 = np.zeros((Q, T))
    f1[np.arange(Q)[:, None], idx4[np.arange(Q) % 128 // 16]] = w
    y = f64(old) + f1
    return y

@@ -1,0 +1,132 @@
+from contextlib import ExitStack
+
+import concourse.mybir as mybir
+
+D, T, I, Q = 512, 1024, 512, 128
+FLOPS = 2 * D * T * Q
+
+F32 = mybir.dt.float32
+BF16 = mybir.dt.bfloat16
+I32 = mybir.dt.int32
+U32 = mybir.dt.uint32
+U16 = mybir.dt.uint16
+U8 = mybir.dt.uint8
+FP8X4 = mybir.dt.float8_e4m3fn_x4
+ALU = mybir.AluOpType
+ACT = mybir.ActivationFunctionType
+
+P = 128
+PACK = 4
+KEY_LOADS = 2
+MM_WIDTHS = (256, 256, 256, 128, 128)
+HALF = I // 2
+LIST_COLS = I // 16
+N_OUT = 256
+
+
+def tile_attend_seconded_lean_putold_heads_kernel(tc, query, keys_words, keys_scales, lam, old, offs, offs2, offs3, offs4, out):
+    nc = tc.nc
+    with ExitStack() as ctx:
+        keep = ctx.enter_context(tc.tile_pool(name="keep", bufs=1))
+        psum = ctx.enter_context(tc.psum_pool(name="psum", bufs=1))
+
+        k_scales = keep.tile([P, T], U8, align_bytes=64)
+        nc.vector.memset(k_scales[:].bitcast(I32), 0)
+        placed = keep.tile([P, T], F32)
+        nc.vector.memset(placed[:], 0.0)
+
+        q_raw = keep.tile([P, PACK, Q], F32)
+        nc.sync.dma_start(out=q_raw[:], in_=query.rearrange("(p j) q -> p j q", j=PACK))
+        for quad in range(4):
+            nc.scalar.dma_start(
+                out=k_scales[32 * quad : 32 * quad + 4, :].bitcast(I32),
+                in_=keys_scales[0, 4 * quad : 4 * quad + 4, :].bitcast(I32),
+            )
+        words = keys_words[0].rearrange("p t r -> p (t r)").bitcast(I32)
+        load_cols = T // KEY_LOADS
+        k_codes = []
+        for c in range(KEY_LOADS):
+            part = keep.tile([P, load_cols], I32, align_bytes=64, name="k_codes%d" % c)
+            nc.sync.dma_start(out=part[:], in_=words[:, c * load_cols : (c + 1) * load_cols])
+            k_codes.append(part)
+
+        lists = {}
+        for name, source in (("opponent", offs3), ("own", offs), ("seconder", offs2), ("place", offs4)):
+            lists[name] = keep.tile([P, LIST_COLS], U16, name="list_" + name)
+            nc.sync.dma_start(lists[name][:], source)
+        lam_col = keep.tile([P, 1], F32)
+        nc.sync.dma_start(out=lam_col[:], in_=lam)
+        totals = keep.tile([P, T], F32)
+        nc.sync.dma_start(out=totals[:], in_=old)
+
+        q_bf16 = keep.tile([P, Q, PACK], BF16, align_bytes=64)
+        q_codes = keep.tile([P, Q], U32, align_bytes=64)
+        q_scales = keep.tile([P, Q], U8, align_bytes=64)
+        q_halves = (slice(0, Q // 2), slice(Q // 2, Q))
+        for rows in q_halves:
+            nc.vector.tensor_copy(out=q_bf16[:, rows, :], in_=q_raw[:, :, rows].rearrange("p j q -> p q j"))
+        for rows in q_halves:
+            nc.vector.quantize_mx(
+                out=q_codes[:, rows].bitcast(FP8X4),
+                scales=q_scales[:, rows],
+                in_=q_bf16[:, rows, :].rearrange("p q j -> p (q j)"),
+            )
+
+        scores = keep.tile([P, T], F32)
+        start = 0
+        for b, width in enumerate(MM_WIDTHS):
+            bank = psum.tile([P, width], F32, name="bank%d" % b)
+            c, first = divmod(start, load_cols)
+            cols = slice(start, start + width)
+            nc.tensor.matmul_mx(
+                out=bank[:],
+                lhsT=q_codes[:].bitcast(FP8X4),
+                lhsT_scale=q_scales[:],
+                rhs=k_codes[c][:, first : first + width].bitcast(FP8X4),
+                rhs_scale=k_scales[:, cols],
+                start=True,
+                stop=True,
+            )
+            if b % 2 == 0:
+                nc.vector.tensor_copy(out=scores[:, cols], in_=bank[:])
+            else:
+                nc.scalar.activation(scores[:, cols], bank[:], ACT.Copy)
+            start += width
+
+        def listed(tile, name, h):
+            return tile[:].indirect(lists[name][:, h * LIST_COLS // 2 : (h + 1) * LIST_COLS // 2])
+
+        opp0 = keep.tile([P, HALF], F32)
+        opp1 = keep.tile([P, HALF], F32)
+        nc.scalar.activation(opp0[:], listed(scores, "opponent", 0), ACT.Copy)
+        nc.scalar.activation(opp1[:], listed(scores, "opponent", 1), ACT.Copy)
+        own0 = keep.tile([P, HALF], F32)
+        nc.vector.tensor_copy(own0[:], listed(scores, "own", 0))
+        gap0 = keep.tile([P, HALF], F32)
+        gap1 = keep.tile([P, HALF], F32)
+        nc.vector.tensor_tensor(gap0[:], listed(scores, "seconder", 0), opp0[:], ALU.subtract)
+        nc.vector.tensor_tensor(gap1[:], listed(scores, "seconder", 1), opp1[:], ALU.subtract)
+
+        lean0 = keep.tile([P, HALF], F32, tag="handed_on")
+        scaled0 = keep.tile([P, HALF], F32)
+        pieces = (slice(0, HALF // 2), slice(HALF // 2, HALF))
+        for cols in pieces:
+            nc.scalar.activation(lean0[:, cols], gap0[:, cols], ACT.Tanh)
+        for cols in pieces:
+            nc.scalar.activation(scaled0[:, cols], lean0[:, cols], ACT.Copy, scale=lam_col[:])
+        nc.vector.tensor_tensor(listed(placed, "place", 0), own0[:], scaled0[:], ALU.add)
+
+        second = keep.tile([P, 2 * HALF], F32, tag="handed_on")
+        lean1, own1 = second[:, :HALF], second[:, HALF:]
+        scaled1 = keep.tile([P, HALF], F32)
+        nc.scalar.activation(lean1, gap1[:], ACT.Tanh)
+        nc.scalar.activation(own1, listed(scores, "own", 1), ACT.Copy)
+        nc.scalar.activation(scaled1[:], lean1, ACT.Copy, scale=lam_col[:])
+        nc.vector.tensor_tensor(listed(placed, "place", 1), own1, scaled1[:], ALU.add)
+
+        for c in range(T // N_OUT):
+            cols = slice(c * N_OUT, (c + 1) * N_OUT)
+            result = keep.tile([P, N_OUT], F32, name="result%d" % c)
+            nc.vector.tensor_tensor(result[:], totals[:, cols], placed[:, cols], ALU.add)
+            queue = nc.sync if c % 2 == 0 else nc.scalar
+            queue.dma_start(out=out[:, cols], in_=result[:])

@@ -21,7 +21,8 @@ KEY_LOADS = 2
 MM_WIDTHS = (256, 256, 256, 128, 128)
 HALF = I // 2
 LIST_COLS = I // 16
-N_OUT = 256
+OUT_WIDTHS = (128, 256, 256, 256, 128)
+PLANE_COLS = T // 4
 
 
 def tile_attend_seconded_lean_putold_heads_kernel(tc, query, keys_words, keys_scales, lam, old, offs, offs2, offs3, offs4, out):
@@ -30,17 +31,16 @@ def tile_attend_seconded_lean_putold_heads_kernel(tc, query, keys_words, keys_sc
         keep = ctx.enter_context(tc.tile_pool(name="keep", bufs=1))
         psum = ctx.enter_context(tc.psum_pool(name="psum", bufs=1))
 
-        k_scales = keep.tile([P, T], U8, align_bytes=64)
-        nc.vector.memset(k_scales[:].bitcast(I32), 0)
+        k_scales = keep.tile([P, PLANE_COLS], U8, align_bytes=64)
         placed = keep.tile([P, T], F32)
         nc.vector.memset(placed[:], 0.0)
 
         q_raw = keep.tile([P, PACK, Q], F32)
         nc.sync.dma_start(out=q_raw[:], in_=query.rearrange("(p j) q -> p j q", j=PACK))
         for quad in range(4):
-            nc.scalar.dma_start(
-                out=k_scales[32 * quad : 32 * quad + 4, :].bitcast(I32),
-                in_=keys_scales[0, 4 * quad : 4 * quad + 4, :].bitcast(I32),
+            nc.sync.dma_start(
+                out=k_scales[32 * quad : 32 * quad + 16, :].bitcast(I32),
+                in_=keys_scales[0, 4 * quad : 4 * quad + 4, :].bitcast(I32).rearrange("r (j c) -> j r c", j=4),
             )
         words = keys_words[0].rearrange("p t r -> p (t r)").bitcast(I32)
         load_cols = T // KEY_LOADS
@@ -59,17 +59,24 @@ def tile_attend_seconded_lean_putold_heads_kernel(tc, query, keys_words, keys_sc
         totals = keep.tile([P, T], F32)
         nc.sync.dma_start(out=totals[:], in_=old)
 
-        q_bf16 = keep.tile([P, Q, PACK], BF16, align_bytes=64)
         q_codes = keep.tile([P, Q], U32, align_bytes=64)
         q_scales = keep.tile([P, Q], U8, align_bytes=64)
         q_halves = (slice(0, Q // 2), slice(Q // 2, Q))
-        for rows in q_halves:
-            nc.vector.tensor_copy(out=q_bf16[:, rows, :], in_=q_raw[:, :, rows].rearrange("p j q -> p q j"))
-        for rows in q_halves:
+        q_bf16 = []
+        for h, rows in enumerate(q_halves):
+            grouped = keep.tile([P, Q // 2, PACK], BF16, align_bytes=64, name="q_bf16_%d" % h)
+            target = grouped[:].rearrange("p (c i) j -> p c j i", i=4)
+            source = q_raw[:, :, rows].rearrange("p j (c i) -> p c j i", i=4)
+            if h == 0:
+                nc.vector.tensor_copy(out=target, in_=source)
+            else:
+                nc.scalar.activation(target, source, ACT.Copy)
+            q_bf16.append(grouped)
+        for h, rows in enumerate(q_halves):
             nc.vector.quantize_mx(
                 out=q_codes[:, rows].bitcast(FP8X4),
                 scales=q_scales[:, rows],
-                in_=q_bf16[:, rows, :].rearrange("p q j -> p (q j)"),
+                in_=q_bf16[h][:].rearrange("p q j -> p (q j)"),
             )
 
         scores = keep.tile([P, T], F32)
@@ -77,13 +84,14 @@ def tile_attend_seconded_lean_putold_heads_kernel(tc, query, keys_words, keys_sc
         for b, width in enumerate(MM_WIDTHS):
             bank = psum.tile([P, width], F32, name="bank%d" % b)
             c, first = divmod(start, load_cols)
+            plane, plane_first = divmod(start, PLANE_COLS)
             cols = slice(start, start + width)
             nc.tensor.matmul_mx(
                 out=bank[:],
                 lhsT=q_codes[:].bitcast(FP8X4),
                 lhsT_scale=q_scales[:],
                 rhs=k_codes[c][:, first : first + width].bitcast(FP8X4),
-                rhs_scale=k_scales[:, cols],
+                rhs_scale=k_scales[4 * plane :, plane_first : plane_first + width],
                 start=True,
                 stop=True,
             )
@@ -124,9 +132,11 @@ def tile_attend_seconded_lean_putold_heads_kernel(tc, query, keys_words, keys_sc
         nc.scalar.activation(scaled1[:], lean1, ACT.Copy, scale=lam_col[:])
         nc.vector.tensor_tensor(listed(placed, "place", 1), own1, scaled1[:], ALU.add)
 
-        for c in range(T // N_OUT):
-            cols = slice(c * N_OUT, (c + 1) * N_OUT)
-            result = keep.tile([P, N_OUT], F32, name="result%d" % c)
+        start = 0
+        for c, width in enumerate(OUT_WIDTHS):
+            cols = slice(start, start + width)
+            result = keep.tile([P, width], F32, name="result%d" % c)
             nc.vector.tensor_tensor(result[:], totals[:, cols], placed[:, cols], ALU.add)
             queue = nc.sync if c % 2 == 0 else nc.scalar
             queue.dma_start(out=out[:, cols], in_=result[:])
+            start += width

from contextlib import ExitStack

import concourse.mybir as mybir

D, T, I, Q = 512, 1024, 512, 128
FLOPS = 2 * D * T * Q

F32 = mybir.dt.float32
BF16 = mybir.dt.bfloat16
I32 = mybir.dt.int32
U32 = mybir.dt.uint32
U16 = mybir.dt.uint16
U8 = mybir.dt.uint8
FP8X4 = mybir.dt.float8_e4m3fn_x4
ALU = mybir.AluOpType
ACT = mybir.ActivationFunctionType

P = 128
PACK = 4
KEY_LOADS = 2
MM_WIDTHS = (256, 256, 256, 128, 128)
HALF = I // 2
LIST_COLS = I // 16
OUT_WIDTHS = (128, 256, 256, 256, 128)
PLANE_COLS = T // 4


def tile_attend_seconded_lean_putold_heads_kernel(tc, query, keys_words, keys_scales, lam, old, offs, offs2, offs3, offs4, out):
    nc = tc.nc
    with ExitStack() as ctx:
        keep = ctx.enter_context(tc.tile_pool(name="keep", bufs=1))
        psum = ctx.enter_context(tc.psum_pool(name="psum", bufs=1))

        k_scales = keep.tile([P, PLANE_COLS], U8, align_bytes=64)
        placed = keep.tile([P, T], F32)
        nc.vector.memset(placed[:], 0.0)

        q_raw = keep.tile([P, PACK, Q], F32)
        nc.sync.dma_start(out=q_raw[:], in_=query.rearrange("(p j) q -> p j q", j=PACK))
        for quad in range(4):
            nc.sync.dma_start(
                out=k_scales[32 * quad : 32 * quad + 16, :].bitcast(I32),
                in_=keys_scales[0, 4 * quad : 4 * quad + 4, :].bitcast(I32).rearrange("r (j c) -> j r c", j=4),
            )
        words = keys_words[0].rearrange("p t r -> p (t r)").bitcast(I32)
        load_cols = T // KEY_LOADS
        k_codes = []
        for c in range(KEY_LOADS):
            part = keep.tile([P, load_cols], I32, align_bytes=64, name="k_codes%d" % c)
            nc.sync.dma_start(out=part[:], in_=words[:, c * load_cols : (c + 1) * load_cols])
            k_codes.append(part)

        lists = {}
        for name, source in (("opponent", offs3), ("own", offs), ("seconder", offs2), ("place", offs4)):
            lists[name] = keep.tile([P, LIST_COLS], U16, name="list_" + name)
            nc.sync.dma_start(lists[name][:], source)
        lam_col = keep.tile([P, 1], F32)
        nc.sync.dma_start(out=lam_col[:], in_=lam)
        totals = keep.tile([P, T], F32)
        nc.sync.dma_start(out=totals[:], in_=old)

        q_codes = keep.tile([P, Q], U32, align_bytes=64)
        q_scales = keep.tile([P, Q], U8, align_bytes=64)
        q_halves = (slice(0, Q // 2), slice(Q // 2, Q))
        q_bf16 = []
        for h, rows in enumerate(q_halves):
            grouped = keep.tile([P, Q // 2, PACK], BF16, align_bytes=64, name="q_bf16_%d" % h)
            target = grouped[:].rearrange("p (c i) j -> p c j i", i=4)
            source = q_raw[:, :, rows].rearrange("p j (c i) -> p c j i", i=4)
            if h == 0:
                nc.vector.tensor_copy(out=target, in_=source)
            else:
                nc.scalar.activation(target, source, ACT.Copy)
            q_bf16.append(grouped)
        for h, rows in enumerate(q_halves):
            nc.vector.quantize_mx(
                out=q_codes[:, rows].bitcast(FP8X4),
                scales=q_scales[:, rows],
                in_=q_bf16[h][:].rearrange("p q j -> p (q j)"),
            )

        scores = keep.tile([P, T], F32)
        start = 0
        for b, width in enumerate(MM_WIDTHS):
            bank = psum.tile([P, width], F32, name="bank%d" % b)
            c, first = divmod(start, load_cols)
            plane, plane_first = divmod(start, PLANE_COLS)
            cols = slice(start, start + width)
            nc.tensor.matmul_mx(
                out=bank[:],
                lhsT=q_codes[:].bitcast(FP8X4),
                lhsT_scale=q_scales[:],
                rhs=k_codes[c][:, first : first + width].bitcast(FP8X4),
                rhs_scale=k_scales[4 * plane :, plane_first : plane_first + width],
                start=True,
                stop=True,
            )
            if b % 2 == 0:
                nc.vector.tensor_copy(out=scores[:, cols], in_=bank[:])
            else:
                nc.scalar.activation(scores[:, cols], bank[:], ACT.Copy)
            start += width

        def listed(tile, name, h):
            return tile[:].indirect(lists[name][:, h * LIST_COLS // 2 : (h + 1) * LIST_COLS // 2])

        opp0 = keep.tile([P, HALF], F32)
        opp1 = keep.tile([P, HALF], F32)
        nc.scalar.activation(opp0[:], listed(scores, "opponent", 0), ACT.Copy)
        nc.scalar.activation(opp1[:], listed(scores, "opponent", 1), ACT.Copy)
        own0 = keep.tile([P, HALF], F32)
        nc.vector.tensor_copy(own0[:], listed(scores, "own", 0))
        gap0 = keep.tile([P, HALF], F32)
        gap1 = keep.tile([P, HALF], F32)
        nc.vector.tensor_tensor(gap0[:], listed(scores, "seconder", 0), opp0[:], ALU.subtract)
        nc.vector.tensor_tensor(gap1[:], listed(scores, "seconder", 1), opp1[:], ALU.subtract)

        lean0 = keep.tile([P, HALF], F32, tag="handed_on")
        scaled0 = keep.tile([P, HALF], F32)
        pieces = (slice(0, HALF // 2), slice(HALF // 2, HALF))
        for cols in pieces:
            nc.scalar.activation(lean0[:, cols], gap0[:, cols], ACT.Tanh)
        for cols in pieces:
            nc.scalar.activation(scaled0[:, cols], lean0[:, cols], ACT.Copy, scale=lam_col[:])
        nc.vector.tensor_tensor(listed(placed, "place", 0), own0[:], scaled0[:], ALU.add)

        second = keep.tile([P, 2 * HALF], F32, tag="handed_on")
        lean1, own1 = second[:, :HALF], second[:, HALF:]
        scaled1 = keep.tile([P, HALF], F32)
        nc.scalar.activation(lean1, gap1[:], ACT.Tanh)
        nc.scalar.activation(own1, listed(scores, "own", 1), ACT.Copy)
        nc.scalar.activation(scaled1[:], lean1, ACT.Copy, scale=lam_col[:])
        nc.vector.tensor_tensor(listed(placed, "place", 1), own1, scaled1[:], ALU.add)

        start = 0
        for c, width in enumerate(OUT_WIDTHS):
            cols = slice(start, start + width)
            result = keep.tile([P, width], F32, name="result%d" % c)
            nc.vector.tensor_tensor(result[:], totals[:, cols], placed[:, cols], ALU.add)
            queue = nc.sync if c % 2 == 0 else nc.scalar
            queue.dma_start(out=out[:, cols], in_=result[:])
            start += width
